import numpy as np
import ml_dtypes


def mxq(x, axis, fmt="e4m3"):
    dtype, down = {"e4m3": (ml_dtypes.float8_e4m3fn, 7), "e5m2": (ml_dtypes.float8_e5m2, 14)}[fmt]
    v = np.moveaxis(np.asarray(x, np.float32).astype(ml_dtypes.bfloat16).astype(np.float64), axis, -1)
    blocks = v.reshape(v.shape[:-1] + (-1, 32))
    amax = np.abs(blocks).max(-1, keepdims=True)
    byte = np.maximum(np.where(amax > 0, np.frexp(amax)[1] - 1 + 127, 0) - down, 1)
    scale = np.exp2(byte - 127.0)
    codes = (blocks / scale).astype(np.float32).astype(dtype).astype(np.float64)
    return np.moveaxis((codes * scale).reshape(v.shape), -1, axis)


WIDE = False


def mx_kscale(k):
    if not WIDE:
        return np.ones(k)
    levels = np.array([10, -10, 5, -5, 0])
    if k % 512:
        return np.exp2(np.random.permutation(np.resize(levels, k // 32))).repeat(32)
    a = np.empty((k // 512, 16))
    for p in range(k // 512):
        a[p, :8] = np.random.permutation(np.resize(levels, 8))
        for g in range(8):
            far = levels[np.abs(levels - a[p, g]) >= 10]
            a[p, g + 8] = far[np.random.randint(len(far))]
    return np.exp2(a.ravel()).repeat(32)


def f64(x):
    return np.asarray(x).astype(np.float64)


def striped(idx):
    return np.tile(idx.reshape(-1, 16).T, (8, 1)).astype(np.uint16)


def unstriped(offs):
    return offs[:16].T.reshape(-1).astype(np.int64)


E2M1 = np.array([0.0, 0.5, 1.0, 1.5, 2.0, 3.0, 4.0, 6.0, -0.0, -0.5, -1.0, -1.5, -2.0, -3.0, -4.0, -6.0])


def pack_weight(w, fmt):
    k, n = w.shape
    w = f64(np.asarray(w, np.float32).astype(ml_dtypes.bfloat16)).reshape(k // 32, 32, n)
    amax = np.abs(w).max(1)
    if fmt == "e4m3":
        byte = np.frexp(amax)[1] - 1 + 127 - 7
    else:
        mant, ex = np.frexp(amax / 6.0)
        byte = np.where(mant > 0.5, ex, ex - 1) + 127
    byte = np.clip(np.where(amax > 0, byte, 1), 1, 254)
    scaled = (w * np.exp2(127.0 - byte)[:, None, :]).reshape(k, n).astype(np.float32)
    by_word = np.ascontiguousarray(scaled.reshape(k // 512, 128, 4, n).transpose(0, 1, 3, 2))
    if fmt == "e4m3":
        words = by_word.astype(ml_dtypes.float8_e4m3fn).view(np.uint8)
    else:
        c = by_word.astype(ml_dtypes.float4_e2m1fn).view(np.uint8) & 0xF
        words = (c[..., 0::2] | (c[..., 1::2] << 4)).reshape(k // 512, 128, 2 * n)
    return np.ascontiguousarray(words), np.ascontiguousarray(byte.astype(np.uint8).reshape(k // 512, 16, n))


def unpack_weight(words, scales, fmt):
    g, _, n = scales.shape
    words = np.ascontiguousarray(words).reshape(g, 128, n, -1)
    if fmt == "e4m3":
        vals = words.view(ml_dtypes.float8_e4m3fn).astype(np.float64)
    else:
        nib = np.empty((g, 128, n, 4), np.uint8)
        nib[..., 0::2] = words & 0xF
        nib[..., 1::2] = words >> 4
        vals = E2M1[nib]
    vals = vals * np.repeat(np.exp2(scales.astype(np.float64) - 127.0), 8, axis=1)[..., None]
    return vals.transpose(0, 1, 3, 2).reshape(g * 512, n)


def gelu(v):
    return 0.5 * v * (1.0 + np.tanh(np.sqrt(2.0 / np.pi) * (v + 0.044715 * v**3)))


K, T, S, H, T2, P = 1024, 2048, 512, 1024, 1024, 512


def setup_inputs():
    n = np.random.standard_normal
    s = mx_kscale(K)[:, None]
    u = mx_kscale(H)[:, None]
    tab_words, tab_scales = pack_weight(n((K, T)) * s, "e4m3")
    w4_words, w4_scales = pack_weight(1.3 * n((K, H)) / np.sqrt(K) / s, "e2m1")
    return {
        "tab_words": tab_words,
        "tab_scales": tab_scales,
        "offs": striped(np.random.permutation(T)[:S]),
        "w4_words": w4_words,
        "w4_scales": w4_scales,
        "gain": (np.exp(0.3 * n(H)) * u[:, 0]).astype(np.float32),
        "wgs": np.exp(0.3 * n((128, S))).astype(np.float32),
        "page0": (n((H, T2)) * u).astype(np.float32),
        "offs2": striped(np.random.permutation(T2)[:S]),
        "offs3": striped(np.random.permutation(T2)[:P]),
        "offs4": striped(np.random.permutation(T2)[:P]),
        "w2": (1.5 * n((H, H)) / np.sqrt(H) / u).astype(np.float32),
    }


def reference(tab_words, tab_scales, offs, w4_words, w4_scales, gain, wgs,
              page0, offs2, offs3, offs4, w2):
    v = unpack_weight(tab_words, tab_scales, "e4m3")[:, unstriped(offs)]
    w4 = unpack_weight(w4_words, w4_scales, "e2m1")
    d = w4.T @ v
    h = f64(gain)[:, None] * np.tanh(d)
    before = f64(page0)
    page = before.copy()
    page[:, unstriped(offs2)] = np.tile(f64(wgs), (H // 128, 1)) * h
    x = page[:, unstriped(offs3)] - np.abs(before[:, unstriped(offs4)])
    xq = mxq(x, 0, "e4m3")
    w2q = mxq(f64(w2), 0, "e4m3")
    return (w2q.T @ xq) + d

@@ -1,0 +1,253 @@
+from contextlib import ExitStack
+
+import concourse.mybir as mybir
+
+K, T, S, H, T2 = 1024, 2048, 512, 1024, 1024
+FLOPS = 2 * K * H * S + 2 * H * H * S
+
+F32 = mybir.dt.float32
+BF16 = mybir.dt.bfloat16
+I32 = mybir.dt.int32
+U32 = mybir.dt.uint32
+U16 = mybir.dt.uint16
+U8 = mybir.dt.uint8
+FP8X4 = mybir.dt.float8_e4m3fn_x4
+FP4X4 = mybir.dt.float4_e2m1fn_x4
+ACT = mybir.ActivationFunctionType
+ALU = mybir.AluOpType
+
+P = 128
+PACK = 4
+PASS = P * PACK
+PASSES = 2
+SLICES = PASSES * PACK
+CHUNKS = ((0, 256), (256, 128), (384, 128))
+
+
+def tile_list_puffin_burrow_census_kernel(
+    tc, tab_words, tab_scales, offs, w4_words, w4_scales, gain, wgs, page0, offs2, offs3, offs4, w2, out
+):
+    nc = tc.nc
+    with ExitStack() as ctx:
+        lists = ctx.enter_context(tc.tile_pool(name="lists", bufs=1))
+        keep = ctx.enter_context(tc.tile_pool(name="keep", bufs=1))
+        ring = ctx.enter_context(tc.tile_pool(name="ring", bufs=2))
+        psum = ctx.enter_context(tc.psum_pool(name="psum", bufs=1))
+
+        def load_list(src, name):
+            tile = lists.tile([P, S // 16], U16, name=name)
+            nc.sync.dma_start(tile[:], src)
+            return tile
+
+        tab_sc = keep.tile([P, PASSES * T], U8, name="tab_sc", align_bytes=64)
+        w4_sc = keep.tile([P, PASSES * H], U8, name="w4_sc", align_bytes=64)
+        nc.vector.memset(tab_sc[:].bitcast(I32), 0)
+        nc.gpsimd.memset(w4_sc[:].bitcast(I32), 0)
+
+        idx = load_list(offs, "idx")
+        idx4 = load_list(offs4, "idx4")
+        idx2 = load_list(offs2, "idx2")
+        idx3 = load_list(offs3, "idx3")
+        gain_sb = keep.tile([P, PASSES, PACK], F32, name="gain_sb")
+        nc.sync.dma_start(gain_sb[:], gain.rearrange("(b p t) -> p b t", b=PASSES, t=PACK))
+        w4_raw = keep.tile([P, PASSES, H // 2], I32, name="w4_raw", align_bytes=64)
+        nc.sync.dma_start(w4_raw[:], w4_words.bitcast(I32).rearrange("a p c -> p a c"))
+        tab = [keep.tile([P, T], I32, name=f"tab{a}", align_bytes=64) for a in range(PASSES)]
+
+        def load_tab(a):
+            nc.sync.dma_start(tab[a][:], tab_words[a].rearrange("p t i -> p (t i)").bitcast(I32))
+
+        load_tab(0)
+        for q in range(4):
+            nc.sync.dma_start(
+                w4_sc[32 * q : 32 * q + 4, :].bitcast(I32).rearrange("r (a t) -> r a t", a=PASSES),
+                w4_scales.bitcast(I32)[:, 4 * q : 4 * q + 4, :].rearrange("a r t -> r a t"),
+            )
+        for q in range(4):
+            nc.sync.dma_start(
+                tab_sc[32 * q : 32 * q + 4, :].bitcast(I32).rearrange("r (a t) -> r a t", a=PASSES),
+                tab_scales.bitcast(I32)[:, 4 * q : 4 * q + 4, :].rearrange("a r t -> r a t"),
+            )
+        load_tab(1)
+
+        page = [keep.tile([P, T2], F32, name=f"page{s}", align_bytes=64) for s in range(SLICES)]
+        page_rows = page0.rearrange("(b p t) c -> b t p c", b=PASSES, t=PACK)
+
+        def load_page(s):
+            nc.sync.dma_start(page[s][:], page_rows[s // PACK, s % PACK])
+
+        wgs_rows = wgs.rearrange("(p t) j -> p t j", t=PACK)
+        wgs_first = keep.tile([P, S], F32, name="wgs_first", align_bytes=64)
+        wgs_rest = keep.tile([P, (PACK - 1) * S], F32, name="wgs_rest", align_bytes=64)
+        wgs_t = [wgs_first[:]] + [wgs_rest[:, t * S : (t + 1) * S] for t in range(PACK - 1)]
+
+        load_page(0)
+        load_page(1)
+        for q in range(4):
+            nc.sync.dma_start(wgs_first[32 * q : 32 * q + 32, :], wgs_rows[:, 0, :])
+        load_page(2)
+        for q in range(4):
+            nc.sync.dma_start(
+                wgs_rest[32 * q : 32 * q + 32, :], wgs_rows[:, 1:PACK, :].rearrange("p t j -> p (t j)")
+            )
+        for s in range(3, SLICES):
+            load_page(s)
+        w2_rows = w2.rearrange("(b p j) n -> b p j n", b=PASSES, j=PACK)
+        w2_raw = {}
+        for b in range(PASSES):
+            for half in range(PASSES):
+                raw = keep.tile([P, PACK, PASS], F32, name=f"w2_raw{b}{half}")
+                nc.sync.dma_start(raw[:], w2_rows[b][:, :, half * PASS : (half + 1) * PASS])
+                w2_raw[b, half] = raw
+
+        w4_dealt = keep.tile([P, PASSES * H * 2], U8, name="w4_dealt", align_bytes=64)
+        w4_sc_dealt = keep.tile([P, PASSES * H], U8, name="w4_sc_dealt", align_bytes=64)
+        words_in = w4_raw[:].bitcast(U16).rearrange("p a (b c i t) -> p b a c t i", b=PASSES, i=8, t=PACK)
+        words_out = w4_dealt[:].bitcast(U16).rearrange(
+            "p (a b t c i) -> p b a c t i", a=PASSES, b=PASSES, t=PACK, i=8
+        )
+        bytes_in = w4_sc[:].rearrange("p (a b c i t) -> p b a c t i", a=PASSES, b=PASSES, i=16, t=PACK)
+        bytes_out = w4_sc_dealt[:].rearrange("p (a b t c i) -> p b a c t i", a=PASSES, b=PASSES, t=PACK, i=16)
+        v_words = [keep.tile([P, S], U32, name=f"v_words{a}", align_bytes=64) for a in range(PASSES)]
+        v_sc = [keep.tile([P, S], U8, name=f"v_sc{a}", align_bytes=64) for a in range(PASSES)]
+        for b in range(PASSES):
+            nc.vector.tensor_copy(words_out[:, b], words_in[:, b])
+        nc.vector.tensor_copy(v_words[0][:], tab[0][:].bitcast(U32).indirect(idx[:]))
+        for b in range(PASSES):
+            nc.vector.tensor_copy(bytes_out[:, b], bytes_in[:, b])
+        for a in range(PASSES):
+            nc.vector.tensor_copy(v_sc[a][:], tab_sc[:, a * T : (a + 1) * T].indirect(idx[:]))
+        nc.vector.tensor_copy(v_words[1][:], tab[1][:].bitcast(U32).indirect(idx[:]))
+
+        d_bank = [psum.tile([P, S], F32, name=f"d_bank{s}", tag=f"bank{s}") for s in range(SLICES)]
+        for s in range(SLICES):
+            for a in range(PASSES):
+                col = a * H + s * P
+                nc.tensor.matmul_mx(
+                    out=d_bank[s][:],
+                    lhsT=w4_dealt[:, 2 * col : 2 * (col + P)].bitcast(FP4X4),
+                    lhsT_scale=w4_sc_dealt[:, col : col + P],
+                    rhs=v_words[a][:].bitcast(FP8X4),
+                    rhs_scale=v_sc[a][:],
+                    start=(a == 0),
+                    stop=(a == PASSES - 1),
+                )
+
+        d = keep.tile([P, SLICES, S], F32, name="d", align_bytes=64)
+        h = [keep.tile([P, S], F32, name=f"h{s}", align_bytes=64) for s in range(SLICES)]
+        size = [keep.tile([P, S], F32, name=f"size{s}", align_bytes=64) for s in range(SLICES)]
+        x_first = keep.tile([P, PACK * S], F32, name="x_first", align_bytes=64)
+        x_wide = keep.tile([P, PACK * CHUNKS[0][1]], F32, name="x_wide", align_bytes=64)
+        x_second = [x_wide[:], h[SLICES - 1][:], wgs_t[PACK - 1]]
+        w2_codes = [keep.tile([P, H], U32, name=f"w2_codes{b}", align_bytes=64) for b in range(PASSES)]
+        w2_sc = [keep.tile([P, H], U8, name=f"w2_sc{b}", align_bytes=64) for b in range(PASSES)]
+
+        def features(s):
+            nc.scalar.activation(h[s][:], d_bank[s][:], ACT.Tanh)
+            nc.scalar.copy(d[:, s, :], d_bank[s][:])
+            nc.scalar.activation(h[s][:], h[s][:], ACT.Copy, scale=gain_sb[:, s // PACK, s % PACK : s % PACK + 1])
+
+        def fetch_before(s):
+            nc.vector.tensor_copy(size[s][:], page[s][:].indirect(idx4[:]))
+
+        def put(s):
+            nc.vector.tensor_tensor(page[s][:].indirect(idx2[:]), h[s][:], wgs_t[s % PACK], ALU.mult)
+
+        def magnitude(s):
+            nc.scalar.activation(size[s][:], size[s][:], ACT.Abs)
+
+        def fetch_after(s, dst, start, width):
+            t = s % PACK
+            nc.vector.tensor_tensor(
+                dst[:, t * width : (t + 1) * width],
+                page[s][:].indirect(idx3[:, start // 16 : (start + width) // 16]),
+                size[s][:, start : start + width],
+                ALU.subtract,
+            )
+
+        def quantise_x(src, width, name):
+            rounded = keep.tile([P, PACK * width], BF16, name=f"{name}_bf", align_bytes=64)
+            nc.scalar.copy(
+                rounded[:].rearrange("p (c i t) -> p c t i", i=4, t=PACK),
+                src.rearrange("p (t c i) -> p c t i", i=4, t=PACK),
+            )
+            codes = keep.tile([P, width], U32, name=f"{name}_codes", align_bytes=64)
+            scales = keep.tile([P, width], U8, name=f"{name}_sc", align_bytes=64)
+            nc.vector.quantize_mx(out=codes[:].bitcast(FP8X4), scales=scales[:], in_=rounded[:])
+            return codes, scales
+
+        def quantise_w2(b, half):
+            rounded = ring.tile([P, PACK * PASS], BF16, name="w2_bf", align_bytes=64)
+            nc.scalar.copy(
+                rounded[:].rearrange("p (t m j) -> p m j t", t=PACK, j=PACK),
+                w2_raw[b, half][:].rearrange("p j (m t) -> p m j t", t=PACK),
+            )
+            cols = slice(half * PASS, (half + 1) * PASS)
+            nc.vector.quantize_mx(out=w2_codes[b][:, cols].bitcast(FP8X4), scales=w2_sc[b][:, cols], in_=rounded[:])
+
+        y_bank = {}
+        first_bank = 0
+        for c, (start, width) in enumerate(CHUNKS):
+            for g in range(SLICES * width // S):
+                y_bank[c, g] = first_bank + g
+            first_bank = first_bank + SLICES * width // S
+        y_tiles = {}
+
+        def product(b, c, codes, scales, col0):
+            start, width = CHUNKS[c]
+            per_bank = S // width
+            for s in range(SLICES):
+                g, place = divmod(s, per_bank)
+                if (c, g) not in y_tiles:
+                    y_tiles[c, g] = psum.tile([P, S], F32, name=f"y_bank{c}{g}", tag=f"bank{y_bank[c, g]}")
+                nc.tensor.matmul_mx(
+                    out=y_tiles[c, g][:, place * width : (place + 1) * width],
+                    lhsT=w2_codes[b][:, s * P : (s + 1) * P].bitcast(FP8X4),
+                    lhsT_scale=w2_sc[b][:, s * P : (s + 1) * P],
+                    rhs=codes[:, col0 : col0 + width].bitcast(FP8X4),
+                    rhs_scale=scales[:, col0 : col0 + width],
+                    start=(b == 0 and place == 0),
+                    stop=(b == PASSES - 1 and place == per_bank - 1),
+                )
+
+        out_rows = out.rearrange("(b p t) j -> p b t j", b=PASSES, t=PACK)
+
+        def finish(c):
+            start, width = CHUNKS[c]
+            per_bank = S // width
+            cols = slice(start, start + width)
+            for g in range(SLICES // per_bank):
+                part = d[:, g * per_bank : (g + 1) * per_bank, cols]
+                nc.vector.tensor_tensor(
+                    part, y_tiles[c, g][:].rearrange("p (s j) -> p s j", s=per_bank), part, ALU.add
+                )
+                b, t = divmod(g * per_bank, PACK)
+                nc.sync.dma_start(out_rows[:, b, t : t + per_bank, cols], part)
+
+        def after(s):
+            magnitude(s)
+            if s < PACK:
+                fetch_after(s, x_first[:], 0, S)
+            else:
+                fetch_after(s, x_second[0], *CHUNKS[0])
+
+        for s in range(SLICES):
+            features(s)
+            fetch_before(s)
+            put(s)
+            if s >= 1:
+                after(s - 1)
+            if s >= PACK:
+                quantise_w2(*divmod(s - PACK, PASSES))
+        codes, scales = quantise_x(x_first[:], S, "x_first")
+        for c, (start, width) in enumerate(CHUNKS):
+            product(0, c, codes, scales, start)
+        after(SLICES - 1)
+        for c, (start, width) in enumerate(CHUNKS):
+            if c > 0:
+                for s in range(PACK, SLICES):
+                    fetch_after(s, x_second[c], start, width)
+            codes, scales = quantise_x(x_second[c], width, f"x_second{c}")
+            product(1, c, codes, scales, 0)
+        for c in range(len(CHUNKS)):
+            finish(c)

@@ -31,7 +31,7 @@ def tile_list_puffin_burrow_census_kernel(
     with ExitStack() as ctx:
         lists = ctx.enter_context(tc.tile_pool(name="lists", bufs=1))
         keep = ctx.enter_context(tc.tile_pool(name="keep", bufs=1))
-        ring = ctx.enter_context(tc.tile_pool(name="ring", bufs=2))
+        ring = ctx.enter_context(tc.tile_pool(name="ring", bufs=4))
         psum = ctx.enter_context(tc.psum_pool(name="psum", bufs=1))
 
         def load_list(src, name):
@@ -44,31 +44,22 @@ def tile_list_puffin_burrow_census_kernel(
         nc.vector.memset(tab_sc[:].bitcast(I32), 0)
         nc.gpsimd.memset(w4_sc[:].bitcast(I32), 0)
 
-        idx = load_list(offs, "idx")
-        idx4 = load_list(offs4, "idx4")
-        idx2 = load_list(offs2, "idx2")
-        idx3 = load_list(offs3, "idx3")
-        gain_sb = keep.tile([P, PASSES, PACK], F32, name="gain_sb")
-        nc.sync.dma_start(gain_sb[:], gain.rearrange("(b p t) -> p b t", b=PASSES, t=PACK))
+        def load_scale_rows(tile, src):
+            for q in range(4):
+                nc.sync.dma_start(
+                    tile[32 * q : 32 * q + 4, :].bitcast(I32).rearrange("r (a c) -> r a c", a=PASSES),
+                    src.bitcast(I32)[:, 4 * q : 4 * q + 4, :].rearrange("a r c -> r a c"),
+                )
+
         w4_raw = keep.tile([P, PASSES, H // 2], I32, name="w4_raw", align_bytes=64)
         nc.sync.dma_start(w4_raw[:], w4_words.bitcast(I32).rearrange("a p c -> p a c"))
+        idx = load_list(offs, "idx")
+        load_scale_rows(tab_sc, tab_scales)
         tab = [keep.tile([P, T], I32, name=f"tab{a}", align_bytes=64) for a in range(PASSES)]
-
-        def load_tab(a):
-            nc.sync.dma_start(tab[a][:], tab_words[a].rearrange("p t i -> p (t i)").bitcast(I32))
-
-        load_tab(0)
-        for q in range(4):
-            nc.sync.dma_start(
-                w4_sc[32 * q : 32 * q + 4, :].bitcast(I32).rearrange("r (a t) -> r a t", a=PASSES),
-                w4_scales.bitcast(I32)[:, 4 * q : 4 * q + 4, :].rearrange("a r t -> r a t"),
-            )
-        for q in range(4):
-            nc.sync.dma_start(
-                tab_sc[32 * q : 32 * q + 4, :].bitcast(I32).rearrange("r (a t) -> r a t", a=PASSES),
-                tab_scales.bitcast(I32)[:, 4 * q : 4 * q + 4, :].rearrange("a r t -> r a t"),
-            )
-        load_tab(1)
+        tab_rows = tab_words.rearrange("a p t i -> a p (t i)").bitcast(I32)
+        nc.sync.dma_start(tab[0][:], tab_rows[0])
+        load_scale_rows(w4_sc, w4_scales)
+        nc.sync.dma_start(tab[1][:], tab_rows[1])
 
         page = [keep.tile([P, T2], F32, name=f"page{s}", align_bytes=64) for s in range(SLICES)]
         page_rows = page0.rearrange("(b p t) c -> b t p c", b=PASSES, t=PACK)
@@ -81,24 +72,29 @@ def tile_list_puffin_burrow_census_kernel(
         wgs_rest = keep.tile([P, (PACK - 1) * S], F32, name="wgs_rest", align_bytes=64)
         wgs_t = [wgs_first[:]] + [wgs_rest[:, t * S : (t + 1) * S] for t in range(PACK - 1)]
 
+        idx4 = load_list(offs4, "idx4")
         load_page(0)
+        gain_sb = keep.tile([P, PASSES, PACK], F32, name="gain_sb")
+        nc.sync.dma_start(gain_sb[:], gain.rearrange("(b p t) -> p b t", b=PASSES, t=PACK))
+        idx2 = load_list(offs2, "idx2")
         load_page(1)
         for q in range(4):
             nc.sync.dma_start(wgs_first[32 * q : 32 * q + 32, :], wgs_rows[:, 0, :])
         load_page(2)
+        idx3 = load_list(offs3, "idx3")
+        load_page(3)
         for q in range(4):
             nc.sync.dma_start(
                 wgs_rest[32 * q : 32 * q + 32, :], wgs_rows[:, 1:PACK, :].rearrange("p t j -> p (t j)")
             )
-        for s in range(3, SLICES):
-            load_page(s)
         w2_rows = w2.rearrange("(b p j) n -> b p j n", b=PASSES, j=PACK)
         w2_raw = {}
-        for b in range(PASSES):
-            for half in range(PASSES):
-                raw = keep.tile([P, PACK, PASS], F32, name=f"w2_raw{b}{half}")
-                nc.sync.dma_start(raw[:], w2_rows[b][:, :, half * PASS : (half + 1) * PASS])
-                w2_raw[b, half] = raw
+        for s in range(PACK, SLICES):
+            b, half = divmod(s - PACK, PASSES)
+            raw = keep.tile([P, PACK, PASS], F32, name=f"w2_raw{b}{half}")
+            nc.sync.dma_start(raw[:], w2_rows[b][:, :, half * PASS : (half + 1) * PASS])
+            w2_raw[b, half] = raw
+            load_page(s)
 
         w4_dealt = keep.tile([P, PASSES * H * 2], U8, name="w4_dealt", align_bytes=64)
         w4_sc_dealt = keep.tile([P, PASSES * H], U8, name="w4_sc_dealt", align_bytes=64)
@@ -112,11 +108,11 @@ def tile_list_puffin_burrow_census_kernel(
         v_sc = [keep.tile([P, S], U8, name=f"v_sc{a}", align_bytes=64) for a in range(PASSES)]
         for b in range(PASSES):
             nc.vector.tensor_copy(words_out[:, b], words_in[:, b])
+        for a in range(PASSES):
+            nc.vector.tensor_copy(v_sc[a][:], tab_sc[:, a * T : (a + 1) * T].indirect(idx[:]))
         nc.vector.tensor_copy(v_words[0][:], tab[0][:].bitcast(U32).indirect(idx[:]))
         for b in range(PASSES):
             nc.vector.tensor_copy(bytes_out[:, b], bytes_in[:, b])
-        for a in range(PASSES):
-            nc.vector.tensor_copy(v_sc[a][:], tab_sc[:, a * T : (a + 1) * T].indirect(idx[:]))
         nc.vector.tensor_copy(v_words[1][:], tab[1][:].bitcast(U32).indirect(idx[:]))
 
         d_bank = [psum.tile([P, S], F32, name=f"d_bank{s}", tag=f"bank{s}") for s in range(SLICES)]
@@ -135,10 +131,17 @@ def tile_list_puffin_burrow_census_kernel(
 
         d = keep.tile([P, SLICES, S], F32, name="d", align_bytes=64)
         h = [keep.tile([P, S], F32, name=f"h{s}", align_bytes=64) for s in range(SLICES)]
-        size = [keep.tile([P, S], F32, name=f"size{s}", align_bytes=64) for s in range(SLICES)]
-        x_first = keep.tile([P, PACK * S], F32, name="x_first", align_bytes=64)
-        x_wide = keep.tile([P, PACK * CHUNKS[0][1]], F32, name="x_wide", align_bytes=64)
-        x_second = [x_wide[:], h[SLICES - 1][:], wgs_t[PACK - 1]]
+        size = keep.tile([P, SLICES, S], F32, name="size", align_bytes=64)
+        picked = [
+            keep.tile([P, PACK, S], F32, name=f"picked{b}", tag=f"picked{b}", align_bytes=64) for b in range(PASSES)
+        ]
+        row = [picked[s // PACK][:, s % PACK, :] for s in range(SLICES)]
+        before = row[: SLICES - 1] + row[:1]
+        x_second = [
+            picked[1][:, :, 0 : CHUNKS[0][1]],
+            h[SLICES - 1][:].rearrange("p (t j) -> p t j", t=PACK),
+            wgs_t[PACK - 1].rearrange("p (t j) -> p t j", t=PACK),
+        ]
         w2_codes = [keep.tile([P, H], U32, name=f"w2_codes{b}", align_bytes=64) for b in range(PASSES)]
         w2_sc = [keep.tile([P, H], U8, name=f"w2_sc{b}", align_bytes=64) for b in range(PASSES)]
 
@@ -148,32 +151,34 @@ def tile_list_puffin_burrow_census_kernel(
             nc.scalar.activation(h[s][:], h[s][:], ACT.Copy, scale=gain_sb[:, s // PACK, s % PACK : s % PACK + 1])
 
         def fetch_before(s):
-            nc.vector.tensor_copy(size[s][:], page[s][:].indirect(idx4[:]))
+            nc.vector.tensor_copy(before[s], page[s][:].indirect(idx4[:]))
 
         def put(s):
             nc.vector.tensor_tensor(page[s][:].indirect(idx2[:]), h[s][:], wgs_t[s % PACK], ALU.mult)
 
         def magnitude(s):
-            nc.scalar.activation(size[s][:], size[s][:], ACT.Abs)
+            nc.scalar.activation(size[:, s, :], before[s], ACT.Abs)
 
         def fetch_after(s, dst, start, width):
-            t = s % PACK
             nc.vector.tensor_tensor(
-                dst[:, t * width : (t + 1) * width],
+                dst,
                 page[s][:].indirect(idx3[:, start // 16 : (start + width) // 16]),
-                size[s][:, start : start + width],
+                size[:, s, start : start + width],
                 ALU.subtract,
             )
 
-        def quantise_x(src, width, name):
-            rounded = keep.tile([P, PACK * width], BF16, name=f"{name}_bf", align_bytes=64)
+        def round_x(src, width, name):
+            rounded = keep.tile([P, PACK * width], BF16, name=name, align_bytes=64)
             nc.scalar.copy(
                 rounded[:].rearrange("p (c i t) -> p c t i", i=4, t=PACK),
-                src.rearrange("p (t c i) -> p c t i", i=4, t=PACK),
+                src.rearrange("p t (c i) -> p c t i", i=4),
             )
-            codes = keep.tile([P, width], U32, name=f"{name}_codes", align_bytes=64)
+            return rounded
+
+        def quantise_x(rounded, width, name, tag):
+            codes = keep.tile([P, width], U32, name=f"{name}_codes", tag=tag, align_bytes=64)
             scales = keep.tile([P, width], U8, name=f"{name}_sc", align_bytes=64)
-            nc.vector.quantize_mx(out=codes[:].bitcast(FP8X4), scales=scales[:], in_=rounded[:])
+            nc.vector.quantize_mx(out=codes[:].bitcast(FP8X4), scales=scales[:], in_=rounded)
             return codes, scales
 
         def quantise_w2(b, half):
@@ -226,28 +231,34 @@ def tile_list_puffin_burrow_census_kernel(
 
         def after(s):
             magnitude(s)
-            if s < PACK:
-                fetch_after(s, x_first[:], 0, S)
-            else:
-                fetch_after(s, x_second[0], *CHUNKS[0])
+            width = S if s < PACK else CHUNKS[0][1]
+            fetch_after(s, row[s][:, 0:width], 0, width)
 
+        wide = CHUNKS[0][1]
         for s in range(SLICES):
             features(s)
+            if s == SLICES - 1:
+                after(s - 1)
+                x_first = round_x(picked[0][:], S, "x_first")
+                codes, scales = quantise_x(x_first[:, 0 : PACK * wide], wide, "x_first_wide", "x_first_wide")
+                product(0, 0, codes, scales, 0)
             fetch_before(s)
             put(s)
-            if s >= 1:
+            if 1 <= s < SLICES - 1:
                 after(s - 1)
-            if s >= PACK:
-                quantise_w2(*divmod(s - PACK, PASSES))
-        codes, scales = quantise_x(x_first[:], S, "x_first")
-        for c, (start, width) in enumerate(CHUNKS):
-            product(0, c, codes, scales, start)
-        after(SLICES - 1)
+            if 3 <= s < SLICES - 1:
+                quantise_w2(*divmod(s - 3, PASSES))
+        magnitude(SLICES - 1)
+        codes, scales = quantise_x(x_first[:, PACK * wide :], S - wide, "x_first_rest", "picked0")
+        for c, (start, width) in enumerate(CHUNKS[1:], 1):
+            product(0, c, codes, scales, start - wide)
+        fetch_after(SLICES - 1, row[SLICES - 1][:, 0:wide], 0, wide)
         for c, (start, width) in enumerate(CHUNKS):
             if c > 0:
                 for s in range(PACK, SLICES):
-                    fetch_after(s, x_second[c], start, width)
-            codes, scales = quantise_x(x_second[c], width, f"x_second{c}")
+                    fetch_after(s, x_second[c][:, s - PACK, :], start, width)
+            rounded = round_x(x_second[c], width, f"x_second{c}")
+            codes, scales = quantise_x(rounded[:], width, f"x_second{c}", f"x_second{c}_codes")
             product(1, c, codes, scales, 0)
         for c in range(len(CHUNKS)):
             finish(c)

from contextlib import ExitStack

import concourse.mybir as mybir

K, T, S, H, T2 = 1024, 2048, 512, 1024, 1024
FLOPS = 2 * K * H * S + 2 * H * H * S

F32 = mybir.dt.float32
BF16 = mybir.dt.bfloat16
I32 = mybir.dt.int32
U32 = mybir.dt.uint32
U16 = mybir.dt.uint16
U8 = mybir.dt.uint8
FP8X4 = mybir.dt.float8_e4m3fn_x4
FP4X4 = mybir.dt.float4_e2m1fn_x4
ACT = mybir.ActivationFunctionType
ALU = mybir.AluOpType

P = 128
PACK = 4
PASS = P * PACK
PASSES = 2
SLICES = PASSES * PACK
CHUNKS = ((0, 256), (256, 128), (384, 128))


def tile_list_puffin_burrow_census_kernel(
    tc, tab_words, tab_scales, offs, w4_words, w4_scales, gain, wgs, page0, offs2, offs3, offs4, w2, out
):
    nc = tc.nc
    with ExitStack() as ctx:
        lists = ctx.enter_context(tc.tile_pool(name="lists", bufs=1))
        keep = ctx.enter_context(tc.tile_pool(name="keep", bufs=1))
        ring = ctx.enter_context(tc.tile_pool(name="ring", bufs=4))
        psum = ctx.enter_context(tc.psum_pool(name="psum", bufs=1))

        def load_list(src, name):
            tile = lists.tile([P, S // 16], U16, name=name)
            nc.sync.dma_start(tile[:], src)
            return tile

        tab_sc = keep.tile([P, PASSES * T], U8, name="tab_sc", align_bytes=64)
        w4_sc = keep.tile([P, PASSES * H], U8, name="w4_sc", align_bytes=64)
        nc.vector.memset(tab_sc[:].bitcast(I32), 0)
        nc.gpsimd.memset(w4_sc[:].bitcast(I32), 0)

        def load_scale_rows(tile, src):
            for q in range(4):
                nc.sync.dma_start(
                    tile[32 * q : 32 * q + 4, :].bitcast(I32).rearrange("r (a c) -> r a c", a=PASSES),
                    src.bitcast(I32)[:, 4 * q : 4 * q + 4, :].rearrange("a r c -> r a c"),
                )

        w4_raw = keep.tile([P, PASSES, H // 2], I32, name="w4_raw", align_bytes=64)
        nc.sync.dma_start(w4_raw[:], w4_words.bitcast(I32).rearrange("a p c -> p a c"))
        idx = load_list(offs, "idx")
        load_scale_rows(tab_sc, tab_scales)
        tab = [keep.tile([P, T], I32, name=f"tab{a}", align_bytes=64) for a in range(PASSES)]
        tab_rows = tab_words.rearrange("a p t i -> a p (t i)").bitcast(I32)
        nc.sync.dma_start(tab[0][:], tab_rows[0])
        load_scale_rows(w4_sc, w4_scales)
        nc.sync.dma_start(tab[1][:], tab_rows[1])

        page = [keep.tile([P, T2], F32, name=f"page{s}", align_bytes=64) for s in range(SLICES)]
        page_rows = page0.rearrange("(b p t) c -> b t p c", b=PASSES, t=PACK)

        def load_page(s):
            nc.sync.dma_start(page[s][:], page_rows[s // PACK, s % PACK])

        wgs_rows = wgs.rearrange("(p t) j -> p t j", t=PACK)
        wgs_first = keep.tile([P, S], F32, name="wgs_first", align_bytes=64)
        wgs_rest = keep.tile([P, (PACK - 1) * S], F32, name="wgs_rest", align_bytes=64)
        wgs_t = [wgs_first[:]] + [wgs_rest[:, t * S : (t + 1) * S] for t in range(PACK - 1)]

        idx4 = load_list(offs4, "idx4")
        load_page(0)
        gain_sb = keep.tile([P, PASSES, PACK], F32, name="gain_sb")
        nc.sync.dma_start(gain_sb[:], gain.rearrange("(b p t) -> p b t", b=PASSES, t=PACK))
        idx2 = load_list(offs2, "idx2")
        load_page(1)
        for q in range(4):
            nc.sync.dma_start(wgs_first[32 * q : 32 * q + 32, :], wgs_rows[:, 0, :])
        load_page(2)
        idx3 = load_list(offs3, "idx3")
        load_page(3)
        for q in range(4):
            nc.sync.dma_start(
                wgs_rest[32 * q : 32 * q + 32, :], wgs_rows[:, 1:PACK, :].rearrange("p t j -> p (t j)")
            )
        w2_rows = w2.rearrange("(b p j) n -> b p j n", b=PASSES, j=PACK)
        w2_raw = {}
        for s in range(PACK, SLICES):
            b, half = divmod(s - PACK, PASSES)
            raw = keep.tile([P, PACK, PASS], F32, name=f"w2_raw{b}{half}")
            nc.sync.dma_start(raw[:], w2_rows[b][:, :, half * PASS : (half + 1) * PASS])
            w2_raw[b, half] = raw
            load_page(s)

        w4_dealt = keep.tile([P, PASSES * H * 2], U8, name="w4_dealt", align_bytes=64)
        w4_sc_dealt = keep.tile([P, PASSES * H], U8, name="w4_sc_dealt", align_bytes=64)
        words_in = w4_raw[:].bitcast(U16).rearrange("p a (b c i t) -> p b a c t i", b=PASSES, i=8, t=PACK)
        words_out = w4_dealt[:].bitcast(U16).rearrange(
            "p (a b t c i) -> p b a c t i", a=PASSES, b=PASSES, t=PACK, i=8
        )
        bytes_in = w4_sc[:].rearrange("p (a b c i t) -> p b a c t i", a=PASSES, b=PASSES, i=16, t=PACK)
        bytes_out = w4_sc_dealt[:].rearrange("p (a b t c i) -> p b a c t i", a=PASSES, b=PASSES, t=PACK, i=16)
        v_words = [keep.tile([P, S], U32, name=f"v_words{a}", align_bytes=64) for a in range(PASSES)]
        v_sc = [keep.tile([P, S], U8, name=f"v_sc{a}", align_bytes=64) for a in range(PASSES)]
        for b in range(PASSES):
            nc.vector.tensor_copy(words_out[:, b], words_in[:, b])
        for a in range(PASSES):
            nc.vector.tensor_copy(v_sc[a][:], tab_sc[:, a * T : (a + 1) * T].indirect(idx[:]))
        nc.vector.tensor_copy(v_words[0][:], tab[0][:].bitcast(U32).indirect(idx[:]))
        for b in range(PASSES):
            nc.vector.tensor_copy(bytes_out[:, b], bytes_in[:, b])
        nc.vector.tensor_copy(v_words[1][:], tab[1][:].bitcast(U32).indirect(idx[:]))

        d_bank = [psum.tile([P, S], F32, name=f"d_bank{s}", tag=f"bank{s}") for s in range(SLICES)]
        for s in range(SLICES):
            for a in range(PASSES):
                col = a * H + s * P
                nc.tensor.matmul_mx(
                    out=d_bank[s][:],
                    lhsT=w4_dealt[:, 2 * col : 2 * (col + P)].bitcast(FP4X4),
                    lhsT_scale=w4_sc_dealt[:, col : col + P],
                    rhs=v_words[a][:].bitcast(FP8X4),
                    rhs_scale=v_sc[a][:],
                    start=(a == 0),
                    stop=(a == PASSES - 1),
                )

        d = keep.tile([P, SLICES, S], F32, name="d", align_bytes=64)
        h = [keep.tile([P, S], F32, name=f"h{s}", align_bytes=64) for s in range(SLICES)]
        size = keep.tile([P, SLICES, S], F32, name="size", align_bytes=64)
        picked = [
            keep.tile([P, PACK, S], F32, name=f"picked{b}", tag=f"picked{b}", align_bytes=64) for b in range(PASSES)
        ]
        row = [picked[s // PACK][:, s % PACK, :] for s in range(SLICES)]
        before = row[: SLICES - 1] + row[:1]
        x_second = [
            picked[1][:, :, 0 : CHUNKS[0][1]],
            h[SLICES - 1][:].rearrange("p (t j) -> p t j", t=PACK),
            wgs_t[PACK - 1].rearrange("p (t j) -> p t j", t=PACK),
        ]
        w2_codes = [keep.tile([P, H], U32, name=f"w2_codes{b}", align_bytes=64) for b in range(PASSES)]
        w2_sc = [keep.tile([P, H], U8, name=f"w2_sc{b}", align_bytes=64) for b in range(PASSES)]

        def features(s):
            nc.scalar.activation(h[s][:], d_bank[s][:], ACT.Tanh)
            nc.scalar.copy(d[:, s, :], d_bank[s][:])
            nc.scalar.activation(h[s][:], h[s][:], ACT.Copy, scale=gain_sb[:, s // PACK, s % PACK : s % PACK + 1])

        def fetch_before(s):
            nc.vector.tensor_copy(before[s], page[s][:].indirect(idx4[:]))

        def put(s):
            nc.vector.tensor_tensor(page[s][:].indirect(idx2[:]), h[s][:], wgs_t[s % PACK], ALU.mult)

        def magnitude(s):
            nc.scalar.activation(size[:, s, :], before[s], ACT.Abs)

        def fetch_after(s, dst, start, width):
            nc.vector.tensor_tensor(
                dst,
                page[s][:].indirect(idx3[:, start // 16 : (start + width) // 16]),
                size[:, s, start : start + width],
                ALU.subtract,
            )

        def round_x(src, width, name):
            rounded = keep.tile([P, PACK * width], BF16, name=name, align_bytes=64)
            nc.scalar.copy(
                rounded[:].rearrange("p (c i t) -> p c t i", i=4, t=PACK),
                src.rearrange("p t (c i) -> p c t i", i=4),
            )
            return rounded

        def quantise_x(rounded, width, name, tag):
            codes = keep.tile([P, width], U32, name=f"{name}_codes", tag=tag, align_bytes=64)
            scales = keep.tile([P, width], U8, name=f"{name}_sc", align_bytes=64)
            nc.vector.quantize_mx(out=codes[:].bitcast(FP8X4), scales=scales[:], in_=rounded)
            return codes, scales

        def quantise_w2(b, half):
            rounded = ring.tile([P, PACK * PASS], BF16, name="w2_bf", align_bytes=64)
            nc.scalar.copy(
                rounded[:].rearrange("p (t m j) -> p m j t", t=PACK, j=PACK),
                w2_raw[b, half][:].rearrange("p j (m t) -> p m j t", t=PACK),
            )
            cols = slice(half * PASS, (half + 1) * PASS)
            nc.vector.quantize_mx(out=w2_codes[b][:, cols].bitcast(FP8X4), scales=w2_sc[b][:, cols], in_=rounded[:])

        y_bank = {}
        first_bank = 0
        for c, (start, width) in enumerate(CHUNKS):
            for g in range(SLICES * width // S):
                y_bank[c, g] = first_bank + g
            first_bank = first_bank + SLICES * width // S
        y_tiles = {}

        def product(b, c, codes, scales, col0):
            start, width = CHUNKS[c]
            per_bank = S // width
            for s in range(SLICES):
                g, place = divmod(s, per_bank)
                if (c, g) not in y_tiles:
                    y_tiles[c, g] = psum.tile([P, S], F32, name=f"y_bank{c}{g}", tag=f"bank{y_bank[c, g]}")
                nc.tensor.matmul_mx(
                    out=y_tiles[c, g][:, place * width : (place + 1) * width],
                    lhsT=w2_codes[b][:, s * P : (s + 1) * P].bitcast(FP8X4),
                    lhsT_scale=w2_sc[b][:, s * P : (s + 1) * P],
                    rhs=codes[:, col0 : col0 + width].bitcast(FP8X4),
                    rhs_scale=scales[:, col0 : col0 + width],
                    start=(b == 0 and place == 0),
                    stop=(b == PASSES - 1 and place == per_bank - 1),
                )

        out_rows = out.rearrange("(b p t) j -> p b t j", b=PASSES, t=PACK)

        def finish(c):
            start, width = CHUNKS[c]
            per_bank = S // width
            cols = slice(start, start + width)
            for g in range(SLICES // per_bank):
                part = d[:, g * per_bank : (g + 1) * per_bank, cols]
                nc.vector.tensor_tensor(
                    part, y_tiles[c, g][:].rearrange("p (s j) -> p s j", s=per_bank), part, ALU.add
                )
                b, t = divmod(g * per_bank, PACK)
                nc.sync.dma_start(out_rows[:, b, t : t + per_bank, cols], part)

        def after(s):
            magnitude(s)
            width = S if s < PACK else CHUNKS[0][1]
            fetch_after(s, row[s][:, 0:width], 0, width)

        wide = CHUNKS[0][1]
        for s in range(SLICES):
            features(s)
            if s == SLICES - 1:
                after(s - 1)
                x_first = round_x(picked[0][:], S, "x_first")
                codes, scales = quantise_x(x_first[:, 0 : PACK * wide], wide, "x_first_wide", "x_first_wide")
                product(0, 0, codes, scales, 0)
            fetch_before(s)
            put(s)
            if 1 <= s < SLICES - 1:
                after(s - 1)
            if 3 <= s < SLICES - 1:
                quantise_w2(*divmod(s - 3, PASSES))
        magnitude(SLICES - 1)
        codes, scales = quantise_x(x_first[:, PACK * wide :], S - wide, "x_first_rest", "picked0")
        for c, (start, width) in enumerate(CHUNKS[1:], 1):
            product(0, c, codes, scales, start - wide)
        fetch_after(SLICES - 1, row[SLICES - 1][:, 0:wide], 0, wide)
        for c, (start, width) in enumerate(CHUNKS):
            if c > 0:
                for s in range(PACK, SLICES):
                    fetch_after(s, x_second[c][:, s - PACK, :], start, width)
            rounded = round_x(x_second[c], width, f"x_second{c}")
            codes, scales = quantise_x(rounded[:], width, f"x_second{c}", f"x_second{c}_codes")
            product(1, c, codes, scales, 0)
        for c in range(len(CHUNKS)):
            finish(c)
